import numpy as np
import ml_dtypes


def mxq(x, axis, fmt="e4m3"):
    dtype, down = {"e4m3": (ml_dtypes.float8_e4m3fn, 7), "e5m2": (ml_dtypes.float8_e5m2, 14)}[fmt]
    v = np.moveaxis(np.asarray(x, np.float32).astype(ml_dtypes.bfloat16).astype(np.float64), axis, -1)
    blocks = v.reshape(v.shape[:-1] + (-1, 32))
    amax = np.abs(blocks).max(-1, keepdims=True)
    byte = np.maximum(np.where(amax > 0, np.frexp(amax)[1] - 1 + 127, 0) - down, 1)
    scale = np.exp2(byte - 127.0)
    codes = (blocks / scale).astype(np.float32).astype(dtype).astype(np.float64)
    return np.moveaxis((codes * scale).reshape(v.shape), -1, axis)


WIDE = False


def mx_kscale(k):
    if not WIDE:
        return np.ones(k)
    levels = np.array([10, -10, 5, -5, 0])
    if k % 512:
        return np.exp2(np.random.permutation(np.resize(levels, k // 32))).repeat(32)
    a = np.empty((k // 512, 16))
    for p in range(k // 512):
        a[p, :8] = np.random.permutation(np.resize(levels, 8))
        for g in range(8):
            far = levels[np.abs(levels - a[p, g]) >= 10]
            a[p, g + 8] = far[np.random.randint(len(far))]
    return np.exp2(a.ravel()).repeat(32)


BF16 = ml_dtypes.bfloat16


def bf(x):
    return np.asarray(x, np.float32).astype(BF16)


def f64(x):
    return np.asarray(x).astype(np.float64)


E2M1 = np.array([0.0, 0.5, 1.0, 1.5, 2.0, 3.0, 4.0, 6.0, -0.0, -0.5, -1.0, -1.5, -2.0, -3.0, -4.0, -6.0])


def pack_weight(w, fmt):
    k, n = w.shape
    w = f64(bf(w)).reshape(k // 32, 32, n)
    amax = np.abs(w).max(1)
    if fmt == "e4m3":
        byte = np.frexp(amax)[1] - 1 + 127 - 7
    else:
        mant, ex = np.frexp(amax / 6.0)
        byte = np.where(mant > 0.5, ex, ex - 1) + 127
    byte = np.clip(np.where(amax > 0, byte, 1), 1, 254)
    scaled = (w * np.exp2(127.0 - byte)[:, None, :]).reshape(k, n).astype(np.float32)
    by_word = np.ascontiguousarray(scaled.reshape(k // 512, 128, 4, n).transpose(0, 1, 3, 2))
    if fmt == "e4m3":
        words = by_word.astype(ml_dtypes.float8_e4m3fn).view(np.uint8)
    else:
        c = by_word.astype(ml_dtypes.float4_e2m1fn).view(np.uint8) & 0xF
        words = c[..., 0::2] | (c[..., 1::2] << 4)
    return np.ascontiguousarray(words), np.ascontiguousarray(byte.astype(np.uint8).reshape(k // 512, 16, n))


def unpack_weight(words, scales, fmt):
    g, p, n, _ = words.shape
    if fmt == "e4m3":
        vals = np.ascontiguousarray(words).view(ml_dtypes.float8_e4m3fn).astype(np.float64)
    else:
        nib = np.empty((g, p, n, 4), np.uint8)
        nib[..., 0::2] = words & 0xF
        nib[..., 1::2] = words >> 4
        vals = E2M1[nib]
    vals = vals * np.repeat(np.exp2(scales.astype(np.float64) - 127.0), 8, axis=1)[..., None]
    return vals.transpose(0, 1, 3, 2).reshape(g * 512, n)
def pack4(w):
    words, scales = pack_weight(w, "e2m1")
    return words.reshape(words.shape[0], 128, -1), scales


def unpack4(words, scales):
    return unpack_weight(words.reshape(words.shape[0], 128, -1, 2), scales, "e2m1")


def planes(Y):
    n, m = Y.shape
    b = f64(bf(Y)).reshape(n // 32, 32, m)
    amax = np.abs(b).max(1)
    byte = np.clip(np.where(amax > 0, np.frexp(amax)[1] - 1 + 127 - 7, 1), 1, 254)
    codes = (b * np.exp2(127.0 - byte)[:, None, :]).reshape(n, m).astype(np.float32).astype(ml_dtypes.float8_e4m3fn).view(np.uint8)
    words = codes.reshape(n // 512, 128, 4, m).transpose(0, 1, 3, 2)
    return np.ascontiguousarray(words), np.ascontiguousarray(byte.astype(np.uint8).reshape(n // 512, 16, m))


N, K, H = 1024, 1024, 512
G = 3 * H


def sigmoid(v):
    return 1.0 / (1.0 + np.exp(-v))


def setup_inputs():
    s = mx_kscale(K)
    u = mx_kscale(N)
    z = bf(np.random.standard_normal((N, K)))
    c = bf(np.random.standard_normal((N, H)))
    w_words, w_scales = pack4(np.random.standard_normal((K, G)) * (1.2 / np.sqrt(K)) / s[:, None])
    return {
        "z": z,
        "c": c,
        "w_words": w_words,
        "w_scales": w_scales,
        "b": bf(np.random.standard_normal(G) * 0.4),
        "a": bf((1.0 + 0.1 * np.random.standard_normal(K)) * s),
        "r": bf((1.0 + 0.1 * np.random.standard_normal(N)) * u),
        "dh_new": bf(np.random.standard_normal((N, H)) / u[:, None]),
    }


def gate_preactivations(z, w, b, a):
    za = z * a[None, :]
    return (mxq(za, 1, "e4m3") @ w) + b[None, :]


def gate_deltas(p, c, dh_new):
    h = c.shape[1]
    pf = p[:, :h]
    pg = p[:, h:2 * h]
    po = p[:, 2 * h:]
    f = sigmoid(pf)
    g = np.tanh(pg)
    o = sigmoid(po)
    tc = np.tanh(f * c + (1.0 - f) * g)
    dct = dh_new * o * (1.0 - tc * tc)
    dpf = dct * (c - g) * f * (1.0 - f)
    dpg = dct * (1.0 - f) * (1.0 - g * g)
    dpo = dh_new * tc * o * (1.0 - o)
    return np.concatenate([dpf, dpg, dpo], axis=-1)


def core(z, c, w_words, w_scales, b, a, r, dh_new):
    z, c, b, a, r, dh_new = f64(z), f64(c), f64(b), f64(a), f64(r), f64(dh_new)
    w = unpack4(w_words, w_scales)
    p = gate_preactivations(z, w, b, a)
    delta = gate_deltas(p, c, dh_new)
    zr = z * r[:, None]
    return mxq(zr, 0, "e4m3").T @ mxq(delta, 0, "e4m3")


def reference(z, c, w_words, w_scales, b, a, r, dh_new):
    R_out = core(z, c, w_words, w_scales, b, a, r, dh_new)
    words, scales = planes(R_out)
    return R_out, words, scales

@@ -1,0 +1,475 @@
+import math
+from contextlib import ExitStack
+
+import concourse.mybir as mybir
+from concourse.masks import make_identity
+
+TOK, CH, HID = 1024, 1024, 512
+GATES = 3 * HID
+P = 128
+FLOPS = 2 * 2 * TOK * CH * GATES
+
+F32 = mybir.dt.float32
+BF16 = mybir.dt.bfloat16
+U32 = mybir.dt.uint32
+I32 = mybir.dt.int32
+U8 = mybir.dt.uint8
+FP8X4 = mybir.dt.float8_e4m3fn_x4
+FP4X4 = mybir.dt.float4_e2m1fn_x4
+ACTF = mybir.ActivationFunctionType
+ALU = mybir.AluOpType
+
+ROOT2 = math.sqrt(2.0)
+ROOT_HALF = math.sqrt(0.5)
+
+GF, GG, GO = 0, 1, 2
+GATE_SCALE = {GF: -0.5, GG: 1.0, GO: 0.5}
+
+
+def tile_coupledlstmfoldedweightgradient_kernel(
+    tc, z, c, w_words, w_scales, b, a, r, dh_new, out_0, out_1, out_2
+):
+    nc = tc.nc
+    with ExitStack() as ctx:
+        keep = ctx.enter_context(tc.tile_pool(name="keep", bufs=1))
+        work = ctx.enter_context(tc.tile_pool(name="work", bufs=2))
+        psum = ctx.enter_context(tc.psum_pool(name="psum", bufs=1))
+        ctx.enter_context(tc.manual_schedule())
+
+        warm = keep.tile([P, 1], F32, name="warm")
+        nc.vector.memset(warm[:], 0.0)
+        warm2 = keep.tile([P, 1], F32, name="warm2")
+        nc.scalar.activation(out=warm2[:], in_=warm[:], func=ACTF.Tanh)
+        ident = keep.tile([P, P], F32, name="ident", align_bytes=64)
+        make_identity(nc, ident[:])
+
+        a_k = keep.tile([P, 2, 4], BF16, name="a_k", align_bytes=64)
+        nc.scalar.dma_start(out=a_k[:], in_=a.rearrange("(k p t) -> p k t", k=2, t=4))
+        z_sb = keep.tile([P, 2, 4, CH], BF16, name="z_sb", align_bytes=64)
+        z_v = z.rearrange("(g p t) k -> g p t k", g=2, t=4)
+        for t in range(4):
+            nc.sync.dma_start(out=z_sb[:, 0, t, :], in_=z_v[0, :, t, :])
+        b_row = keep.tile([P, P], BF16, name="b_row", align_bytes=64)
+        nc.vector.memset(b_row[:], 0.0)
+        nc.scalar.dma_start(out=b_row[0:12, :], in_=b.rearrange("(c h) -> c h", c=12))
+        wsc = keep.tile([P, 2, GATES], U8, name="wsc", align_bytes=64)
+        nc.vector.memset(wsc[:].rearrange("p k n -> p (k n)").bitcast(I32), 0)
+        for q in range(4):
+            nc.scalar.dma_start(
+                out=wsc[32 * q : 32 * q + 4, :, :].bitcast(I32),
+                in_=w_scales[:, 4 * q : 4 * q + 4, :].rearrange("k r n -> r k n").bitcast(I32),
+            )
+        r_t = keep.tile([P, 2, 4], BF16, name="r_t", align_bytes=64)
+        nc.scalar.dma_start(out=r_t[:], in_=r.rearrange("(g p t) -> p g t", g=2, t=4))
+        w_sb = keep.tile([P, 2, 2 * GATES], U8, name="w_sb", align_bytes=64)
+        nc.sync.dma_start(out=w_sb[:].bitcast(I32), in_=w_words.rearrange("k p n -> p k n").bitcast(I32))
+        c_sb = keep.tile([P, 2, 4, HID], BF16, name="c_sb", align_bytes=64)
+        dh_sb = keep.tile([P, 2, 4, HID], BF16, name="dh_sb", align_bytes=64)
+        c_v = c.rearrange("(g p t) h -> g p t h", g=2, t=4)
+        dh_v = dh_new.rearrange("(g p t) h -> g p t h", g=2, t=4)
+        for t in range(4):
+            nc.sync.dma_start(out=z_sb[:, 1, t, :], in_=z_v[1, :, t, :])
+        nc.sync.dma_start(out=c_sb[:, 0], in_=c_v[0])
+        nc.sync.dma_start(out=dh_sb[:, 0], in_=dh_v[0])
+        nc.sync.dma_start(out=c_sb[:, 1], in_=c_v[1])
+        nc.sync.dma_start(out=dh_sb[:, 1], in_=dh_v[1])
+
+        ident_b = keep.tile([P, P], BF16, name="ident_b", align_bytes=64)
+        nc.vector.tensor_copy(out=ident_b[:], in_=ident[:])
+
+        a_bc = keep.tile([P, 2, CH // 2], BF16, name="a_bc", align_bytes=64)
+        for u in range(2):
+            a_ps = psum.tile([P, 512], BF16, name="a_ps", tag="s2", bufs=3)
+            for kg in range(2):
+                for e in range(2):
+                    j = 2 * kg + e
+                    nc.tensor.transpose(
+                        a_ps[:, j * P : (j + 1) * P],
+                        a_k[:, kg, 2 * u + e : 2 * u + e + 1].to_broadcast([P, P]),
+                        ident_b[:],
+                    )
+            a_out = a_bc[:, u, :].rearrange("p (k w e) -> p k w e", k=2, e=2)
+            a_in = a_ps[:].rearrange("p (k e w) -> p k w e", k=2, e=2)
+            if u == 0:
+                nc.vector.tensor_copy(out=a_out, in_=a_in)
+            else:
+                nc.scalar.copy(out=a_out, in_=a_in)
+
+        bias = keep.tile([P, 12], F32, name="bias")
+
+        def make_bias():
+            b_ps = psum.tile([P, P], BF16, name="b_ps", tag="s2", bufs=3)
+            nc.tensor.transpose(b_ps[:], b_row[:], ident_b[:])
+            for gate in (GF, GG, GO):
+                cols = slice(4 * gate, 4 * gate + 4)
+                nc.vector.tensor_scalar_mul(out=bias[:, cols], in0=b_ps[:, cols], scalar1=GATE_SCALE[gate])
+
+        zaq = [keep.tile([P, 2, 512], U32, name="zaq%d" % g, align_bytes=64) for g in range(2)]
+        zas = [keep.tile([P, 2, 512], U8, name="zas%d" % g, align_bytes=64) for g in range(2)]
+        zrq = [keep.tile([P, CH], U32, name="zrq%d" % g, align_bytes=64) for g in range(2)]
+        zrs = [keep.tile([P, CH], U8, name="zrs%d" % g, align_bytes=64) for g in range(2)]
+        osc = keep.tile([P, 2, GATES], U8, name="osc", align_bytes=64)
+        r_f = keep.tile([P, 8], F32, name="r_f")
+        zag = {}
+        zrn = {}
+
+        def za_mul(g, t):
+            za = work.tile([P, 2, CH // 2], BF16, name="za", bufs=4, align_bytes=64)
+            nc.vector.tensor_tensor(
+                out=za[:].rearrange("p u (w e) -> p u w e", e=2),
+                in0=z_sb[:, g, t, :].rearrange("p (w u e) -> p u w e", u=2, e=2),
+                in1=a_bc[:].rearrange("p u (w e) -> p u w e", e=2),
+                op=ALU.mult,
+            )
+            return za
+
+        def za_turn(g, t, za, copy):
+            half, s = divmod(t, 2)
+            if (g, half) not in zag:
+                zag[g, half] = work.tile([P, 2, 256 * 4], BF16, name="zag", bufs=4, align_bytes=64)
+            words = za[:].rearrange("p u x -> p (u x)").bitcast(F32)
+            ps = psum.tile([P, 512], F32, name="zt_ps", tag="s2", bufs=3)
+            for kg in range(2):
+                for u in range(2):
+                    j = 2 * kg + u
+                    nc.tensor.transpose(
+                        ps[:, j * P : (j + 1) * P],
+                        words[:, 256 * u + P * kg : 256 * u + P * (kg + 1)],
+                        ident[:],
+                    )
+            dst = zag[g, half][:].rearrange("p k x -> p (k x)").bitcast(F32).rearrange("p (k n u) -> p k n u", k=2, u=2)
+            copy(
+                out=dst[:, :, s * P : (s + 1) * P, :],
+                in_=ps[:].rearrange("p (k u n) -> p k n u", k=2, u=2),
+            )
+
+        def za_quant(g, half):
+            for kg in range(2):
+                cols = slice(256 * half, 256 * half + 256)
+                nc.vector.quantize_mx(
+                    out=zaq[g][:, kg, cols].bitcast(FP8X4), scales=zas[g][:, kg, cols], in_=zag[g, half][:, kg, :]
+                )
+
+        def zr_scale(g, t):
+            if g not in zrn:
+                zrn[g] = work.tile([P, 4, CH], BF16, name="zrn", bufs=1, align_bytes=64)
+            nc.scalar.activation(
+                out=zrn[g][:, t, :].rearrange("p (k s m) -> p k s m", k=2, s=4),
+                in_=z_sb[:, g, t, :].rearrange("p (k m s) -> p k s m", k=2, s=4),
+                func=ACTF.Copy,
+                scale=r_f[:, 4 * g + t : 4 * g + t + 1],
+            )
+
+        def zr_mul(g, G):
+            zr = work.tile([P, 512 * 4], BF16, name="zr", bufs=2, align_bytes=64)
+            nc.vector.tensor_tensor(
+                out=zr[:].rearrange("p (s m t) -> p s m t", s=4, t=4),
+                in0=z_sb[:, g, :, 512 * G : 512 * G + 512].rearrange("p t (m s) -> p s m t", s=4),
+                in1=r_t[:, g, :].unsqueeze(1).unsqueeze(1).to_broadcast([P, 4, P, 4]),
+                op=ALU.mult,
+            )
+            return zr
+
+        def zr_join(g, G):
+            zr = work.tile([P, 512 * 4], BF16, name="zr", bufs=2, align_bytes=64)
+            nc.vector.tensor_copy(
+                out=zr[:].rearrange("p (c t) -> p c t", t=4),
+                in_=zrn[g][:, :, 512 * G : 512 * G + 512].rearrange("p t c -> p c t"),
+            )
+            return zr
+
+        def zr_quant(g, G, zr):
+            cols = slice(512 * G, 512 * G + 512)
+            nc.vector.quantize_mx(out=zrq[g][:, cols].bitcast(FP8X4), scales=zrs[g][:, cols], in_=zr[:])
+
+        acts = {}
+        turned = {}
+        vals = {}
+        deltas = {}
+        marks = {}
+
+        def gate_mm(i, gate):
+            hc, g = divmod(i, 2)
+            col = gate * HID + hc * P
+            mm = psum.tile([P, 512], F32, name="s1_ps", tag="s1", bufs=2)
+            for kg in range(2):
+                nc.tensor.matmul_mx(
+                    out=mm[:],
+                    lhsT=w_sb[:, kg, 2 * col : 2 * col + 256].bitcast(FP4X4),
+                    lhsT_scale=wsc[:, kg, col : col + P],
+                    rhs=zaq[g][:, kg, :].bitcast(FP8X4),
+                    rhs_scale=zas[g][:, kg, :],
+                    start=(kg == 0),
+                    stop=(kg == 1),
+                )
+            act = work.tile([P, 512], F32, name="act%d" % gate, bufs=2, align_bytes=64)
+            nc.scalar.activation(
+                out=act[:],
+                in_=mm[:],
+                func=ACTF.Tanh,
+                bias=bias[:, 4 * gate + hc : 4 * gate + hc + 1],
+                scale=GATE_SCALE[gate],
+            )
+            acts[i, gate] = act
+
+        def gates(i):
+            for gate in (GG, GO, GF):
+                gate_mm(i, gate)
+
+        def turn_gate(i, gate):
+            tp = psum.tile([P, 512], F32, name="tp%d" % gate, tag="tp%d" % gate, bufs=1)
+            for t in range(4):
+                nc.tensor.transpose(tp[:, t * P : (t + 1) * P], acts[i, gate][:, t * P : (t + 1) * P], ident[:])
+            turned[i, gate] = tp[:].rearrange("p (t h) -> p h t", t=4)
+
+        def turn(i):
+            for gate in (GG, GO, GF):
+                turn_gate(i, gate)
+
+        def new(i, name):
+            v = work.tile([P, 512], F32, name=name, bufs=2, align_bytes=64)
+            vals[i, name] = v
+            return v[:].rearrange("p (h t) -> p h t", t=4)
+
+        def ht(i, name):
+            return vals[i, name][:].rearrange("p (h t) -> p h t", t=4)
+
+        def square_g(i):
+            nc.scalar.activation(out=new(i, "g2"), in_=turned[i, GG], func=ACTF.Square, scale=ROOT2)
+
+        def phase_a(i):
+            hc, g = divmod(i, 2)
+            cols = slice(hc * P, hc * P + P)
+            c_ht = c_sb[:, g, :, cols].rearrange("p t h -> p h t")
+            dh_ht = dhq[:, g, :, cols].rearrange("p t h -> p h t")
+            f_, g_, o_ = turned[i, GF], turned[i, GG], turned[i, GO]
+            stt = nc.vector.scalar_tensor_tensor
+            nc.vector.tensor_tensor(out=new(i, "d"), in0=c_ht, in1=g_, op=ALU.subtract)
+            stt(out=new(i, "do"), in0=o_, scalar=1.0, in1=dh_ht, op0=ALU.add, op1=ALU.mult)
+            stt(out=new(i, "w"), in0=f_, scalar=1.0, in1=ht(i, "d"), op0=ALU.subtract, op1=ALU.mult)
+            stt(out=new(i, "t1"), in0=o_, scalar=1.0, in1=ht(i, "do"), op0=ALU.subtract, op1=ALU.mult)
+            stt(out=new(i, "s"), in0=ht(i, "w"), scalar=0.5, in1=g_, op0=ALU.mult, op1=ALU.subtract)
+            stt(out=new(i, "e"), in0=f_, scalar=1.0, in1=ht(i, "do"), op0=ALU.add, op1=ALU.mult)
+
+        def cell_tanh(i):
+            new(i, "tc")
+            nc.scalar.activation(out=vals[i, "tc"][:], in_=vals[i, "s"][:], func=ACTF.Tanh)
+
+        def cell_square(i):
+            new(i, "sq")
+            nc.scalar.activation(out=vals[i, "sq"][:], in_=vals[i, "tc"][:], func=ACTF.Square, scale=ROOT_HALF)
+
+        def delta_quant(i, gate, src):
+            codes, scales = deltas[i]
+            cols = slice(gate * P, gate * P + P)
+            nc.vector.quantize_mx(out=codes[:, cols].bitcast(FP8X4), scales=scales[:, cols], in_=src[:])
+
+        def phase_y(i):
+            new(i, "y")
+            nc.vector.scalar_tensor_tensor(
+                out=vals[i, "y"][:], in0=vals[i, "sq"][:], scalar=0.5, in1=vals[i, "e"][:], op0=ALU.subtract, op1=ALU.mult
+            )
+
+        def delta_o(i, eng):
+            dpo = work.tile([P, 512], BF16, name="dpo", bufs=2, align_bytes=64)
+            eng.tensor_tensor(out=dpo[:], in0=vals[i, "t1"][:], in1=vals[i, "tc"][:], op=ALU.mult)
+            return dpo
+
+        def delta_f(i, eng):
+            dpf = work.tile([P, 512], BF16, name="dpf", bufs=2, align_bytes=64)
+            eng.tensor_tensor(out=dpf[:], in0=vals[i, "y"][:], in1=vals[i, "w"][:], op=ALU.mult)
+            return dpf
+
+        def delta_g(i):
+            dpg = work.tile([P, 512], BF16, name="dpg", bufs=2, align_bytes=64)
+            nc.vector.scalar_tensor_tensor(
+                out=dpg[:], in0=vals[i, "g2"][:], scalar=2.0, in1=vals[i, "y"][:], op0=ALU.subtract, op1=ALU.mult
+            )
+            return dpg
+
+        def delta_tiles(i):
+            codes = work.tile([P, 3 * P], U32, name="dq", bufs=4, align_bytes=64)
+            scales = work.tile([P, 3 * P], U8, name="dqs", bufs=4, align_bytes=64)
+            deltas[i] = (codes, scales)
+
+        gp = {}
+
+        def phase_y_and_gp(i):
+            phase_y(i)
+            gp[i] = (delta_o(i, nc.gpsimd), delta_f(i, nc.gpsimd))
+
+        def phase_b(i, fill):
+            delta_tiles(i)
+            dpo, dpf = gp[i]
+            dpg = delta_g(i)
+            for cast, plane in fill:
+                cast()
+            delta_quant(i, GO, dpo)
+            delta_quant(i, GF, dpf)
+            for cast, plane in fill[:1]:
+                plane()
+            delta_quant(i, GG, dpg)
+            for cast, plane in fill[1:]:
+                plane()
+
+        def phase_b_last(i):
+            delta_tiles(i)
+            dpo = delta_o(i, nc.vector)
+            phase_y(i)
+            delta_quant(i, GO, dpo)
+            dpg = delta_g(i)
+            dpf = delta_f(i, nc.vector)
+            delta_quant(i, GG, dpg)
+            delta_quant(i, GF, dpf)
+
+        ow = {}
+        done = {}
+        pending = []
+
+        def store_words(hc, G):
+            dst = out_1[G].rearrange("p m b -> p (m b)").bitcast(I32).rearrange("p (s m) -> p s m", s=3)
+            nc.sync.dma_start(
+                out=dst[:, :, hc * P : hc * P + P],
+                in_=ow[hc, G][:].bitcast(I32).rearrange("p (s m) -> p s m", s=3),
+            )
+
+        def out_bank(hc, G, gate, how):
+            col = gate * HID + hc * P
+            mm = psum.tile([P, 512], F32, name="s2_ps", tag="s2", bufs=3)
+            for t in range(4):
+                ch = slice(512 * G + P * t, 512 * G + P * t + P)
+                for g in range(2):
+                    codes, scales = deltas[2 * hc + g]
+                    nc.tensor.matmul_mx(
+                        out=mm[:, P * t : P * t + P],
+                        lhsT=zrq[g][:, ch].bitcast(FP8X4),
+                        lhsT_scale=zrs[g][:, ch],
+                        rhs=codes[:, gate * P : gate * P + P].bitcast(FP8X4),
+                        rhs_scale=scales[:, gate * P : gate * P + P],
+                        start=(g == 0),
+                        stop=(g == 1),
+                    )
+            res = work.tile([P, 512], F32, name="res", bufs=6, align_bytes=64)
+            nc.scalar.copy(out=res[:], in_=mm[:])
+            nc.sync.dma_start(
+                out=out_0[512 * G : 512 * G + 512, col : col + P].rearrange("(p t) m -> p t m", t=4),
+                in_=res[:].rearrange("p (t m) -> p t m", t=4),
+            )
+            og = work.tile([P, 512], BF16, name="og", bufs=6, align_bytes=64)
+            og_v = og[:].rearrange("p (m t) -> p m t", t=4)
+            if how == "A":
+                nc.scalar.copy(out=og_v, in_=mm[:].rearrange("p (t m) -> p m t", t=4))
+            if (hc, G) not in ow:
+                ow[hc, G] = work.tile([P, 3 * P], U32, name="ow", bufs=4, align_bytes=64)
+                done[hc, G] = 0
+            words = ow[hc, G]
+
+            def cast():
+                if how == "V":
+                    nc.vector.tensor_copy(out=og_v, in_=res[:].rearrange("p (t m) -> p m t", t=4))
+
+            def plane():
+                nc.vector.quantize_mx(
+                    out=words[:, gate * P : gate * P + P].bitcast(FP8X4),
+                    scales=osc[:, G, col : col + P],
+                    in_=og[:],
+                )
+                done[hc, G] += 1
+                if done[hc, G] == 3:
+                    store_words(hc, G)
+
+            pending.append((cast, plane))
+
+        def take_pending(n=99):
+            got = list(pending[:n])
+            rest = list(pending[n:])
+            pending.clear()
+            pending.extend(rest)
+            return got
+
+        VC, AC = nc.vector.tensor_copy, nc.scalar.copy
+        dhq = keep.tile([P, 2, 4, HID], BF16, name="dhq", align_bytes=64)
+
+        def quarter_dh(g):
+            nc.vector.tensor_scalar_mul(out=dhq[:, g], in0=dh_sb[:, g], scalar1=0.25)
+
+        tiles = [za_mul(0, t) for t in range(4)]
+        for t in range(4):
+            za_turn(0, t, tiles[t], VC if t == 2 else AC)
+        make_bias()
+        nc.vector.tensor_copy(out=r_f[:], in_=r_t[:].rearrange("p g t -> p (g t)"))
+        za_quant(0, 0)
+        za_quant(0, 1)
+        gates(0)
+        zr00 = zr_mul(0, 0)
+        tiles = [za_mul(1, t) for t in range(4)]
+        turn(0)
+        square_g(0)
+        quarter_dh(0)
+        phase_a(0)
+        for t in range(4):
+            za_turn(1, t, tiles[t], AC)
+        cell_tanh(0)
+        cell_square(0)
+        za_quant(1, 0)
+        zr_quant(0, 0, zr00)
+        za_quant(1, 1)
+        gates(1)
+        zr01 = zr_mul(0, 1)
+        turn(1)
+        square_g(1)
+        zr_scale(1, 0)
+        quarter_dh(1)
+
+        hows = "VVAVVA"
+        for i in range(1, 8):
+            phase_y_and_gp(i - 1)
+            if i < 7:
+                gates(i + 1)
+            phase_a(i)
+            if i == 1:
+                zr_quant(0, 1, zr01)
+            if i == 2:
+                zr10 = zr_join(1, 0)
+                zr11 = zr_join(1, 1)
+            phase_b(i - 1, take_pending())
+            if i == 2:
+                zr_quant(1, 0, zr10)
+                zr_quant(1, 1, zr11)
+            banks = []
+            if i >= 3:
+                hc, G = divmod(i - 3, 2)
+                banks = [(hc, G, gate) for gate in (GO, GG, GF)]
+            if i == 7:
+                banks += [(hc, 1, gate) for gate in (GO, GG, GF)]
+            if banks:
+                out_bank(*banks[0], hows[0])
+            cell_tanh(i)
+            cell_square(i)
+            if i < 7:
+                turn(i + 1)
+                square_g(i + 1)
+            if i == 1:
+                for t in range(1, 4):
+                    zr_scale(1, t)
+            for k in range(1, len(banks)):
+                out_bank(*banks[k], hows[k])
+        fill = take_pending()
+        for cast, plane in fill:
+            cast()
+        phase_b_last(7)
+        for cast, plane in fill:
+            plane()
+        for gate in (GO, GG, GF):
+            for G in range(2):
+                out_bank(3, G, gate, "V" if G else "A")
+            fill = take_pending()
+            for cast, plane in fill:
+                cast()
+            for cast, plane in fill:
+                plane()
+        for q in range(4):
+            nc.sync.dma_start(
+                out=out_2[:, 4 * q : 4 * q + 4, :].rearrange("g r m -> r g m").bitcast(I32),
+                in_=osc[32 * q : 32 * q + 4, :, :].bitcast(I32),
+            )

@@ -296,7 +296,8 @@ def tile_coupledlstmfoldedweightgradient_kernel(
 
         def phase_y_and_gp(i):
             phase_y(i)
-            gp[i] = (delta_o(i, nc.gpsimd), delta_f(i, nc.gpsimd))
+            dpf = delta_f(i, nc.gpsimd)
+            gp[i] = (delta_o(i, nc.gpsimd), dpf)
 
         def phase_b(i, fill):
             delta_tiles(i)

@@ -22,7 +22,7 @@ ALU = mybir.AluOpType
 ROOT2 = math.sqrt(2.0)
 ROOT_HALF = math.sqrt(0.5)
 
-GF, GG, GO = 0, 1, 2
+GF, GG, GO, GSQ = 0, 1, 2, 3
 GATE_SCALE = {GF: -0.5, GG: 1.0, GO: 0.5}
 
 
@@ -45,6 +45,8 @@ def tile_coupledlstmfoldedweightgradient_kernel(
 
         a_k = keep.tile([P, 2, 4], BF16, name="a_k", align_bytes=64)
         nc.scalar.dma_start(out=a_k[:], in_=a.rearrange("(k p t) -> p k t", k=2, t=4))
+        r_t = keep.tile([P, 2, 4], BF16, name="r_t", align_bytes=64)
+        nc.scalar.dma_start(out=r_t[:], in_=r.rearrange("(g p t) -> p g t", g=2, t=4))
         z_sb = keep.tile([P, 2, 4, CH], BF16, name="z_sb", align_bytes=64)
         z_v = z.rearrange("(g p t) k -> g p t k", g=2, t=4)
         for t in range(4):
@@ -59,46 +61,31 @@ def tile_coupledlstmfoldedweightgradient_kernel(
                 out=wsc[32 * q : 32 * q + 4, :, :].bitcast(I32),
                 in_=w_scales[:, 4 * q : 4 * q + 4, :].rearrange("k r n -> r k n").bitcast(I32),
             )
-        r_t = keep.tile([P, 2, 4], BF16, name="r_t", align_bytes=64)
-        nc.scalar.dma_start(out=r_t[:], in_=r.rearrange("(g p t) -> p g t", g=2, t=4))
-        w_sb = keep.tile([P, 2, 2 * GATES], U8, name="w_sb", align_bytes=64)
-        nc.sync.dma_start(out=w_sb[:].bitcast(I32), in_=w_words.rearrange("k p n -> p k n").bitcast(I32))
+        w_sb = {}
+        for gate in (GG, GO, GF):
+            w_sb[gate] = keep.tile([P, 2, 2 * HID], U8, name="w_sb%d" % gate, align_bytes=64)
+            nc.sync.dma_start(
+                out=w_sb[gate][:].bitcast(I32),
+                in_=w_words[:, :, 2 * gate * HID : 2 * (gate + 1) * HID].rearrange("k p n -> p k n").bitcast(I32),
+            )
         c_sb = keep.tile([P, 2, 4, HID], BF16, name="c_sb", align_bytes=64)
         dh_sb = keep.tile([P, 2, 4, HID], BF16, name="dh_sb", align_bytes=64)
         c_v = c.rearrange("(g p t) h -> g p t h", g=2, t=4)
         dh_v = dh_new.rearrange("(g p t) h -> g p t h", g=2, t=4)
-        for t in range(4):
-            nc.sync.dma_start(out=z_sb[:, 1, t, :], in_=z_v[1, :, t, :])
         nc.sync.dma_start(out=c_sb[:, 0], in_=c_v[0])
         nc.sync.dma_start(out=dh_sb[:, 0], in_=dh_v[0])
+        for t in range(4):
+            nc.sync.dma_start(out=z_sb[:, 1, t, :], in_=z_v[1, :, t, :])
         nc.sync.dma_start(out=c_sb[:, 1], in_=c_v[1])
         nc.sync.dma_start(out=dh_sb[:, 1], in_=dh_v[1])
 
         ident_b = keep.tile([P, P], BF16, name="ident_b", align_bytes=64)
         nc.vector.tensor_copy(out=ident_b[:], in_=ident[:])
 
-        a_bc = keep.tile([P, 2, CH // 2], BF16, name="a_bc", align_bytes=64)
-        for u in range(2):
-            a_ps = psum.tile([P, 512], BF16, name="a_ps", tag="s2", bufs=3)
-            for kg in range(2):
-                for e in range(2):
-                    j = 2 * kg + e
-                    nc.tensor.transpose(
-                        a_ps[:, j * P : (j + 1) * P],
-                        a_k[:, kg, 2 * u + e : 2 * u + e + 1].to_broadcast([P, P]),
-                        ident_b[:],
-                    )
-            a_out = a_bc[:, u, :].rearrange("p (k w e) -> p k w e", k=2, e=2)
-            a_in = a_ps[:].rearrange("p (k e w) -> p k w e", k=2, e=2)
-            if u == 0:
-                nc.vector.tensor_copy(out=a_out, in_=a_in)
-            else:
-                nc.scalar.copy(out=a_out, in_=a_in)
-
         bias = keep.tile([P, 12], F32, name="bias")
 
         def make_bias():
-            b_ps = psum.tile([P, P], BF16, name="b_ps", tag="s2", bufs=3)
+            b_ps = psum.tile([P, P], BF16, name="b_ps", tag="s2", bufs=2)
             nc.tensor.transpose(b_ps[:], b_row[:], ident_b[:])
             for gate in (GF, GG, GO):
                 cols = slice(4 * gate, 4 * gate + 4)
@@ -113,35 +100,29 @@ def tile_coupledlstmfoldedweightgradient_kernel(
         zag = {}
         zrn = {}
 
-        def za_mul(g, t):
-            za = work.tile([P, 2, CH // 2], BF16, name="za", bufs=4, align_bytes=64)
-            nc.vector.tensor_tensor(
-                out=za[:].rearrange("p u (w e) -> p u w e", e=2),
-                in0=z_sb[:, g, t, :].rearrange("p (w u e) -> p u w e", u=2, e=2),
-                in1=a_bc[:].rearrange("p u (w e) -> p u w e", e=2),
-                op=ALU.mult,
-            )
-            return za
-
-        def za_turn(g, t, za, copy):
+        def za_turn(g, t, tag, bufs):
             half, s = divmod(t, 2)
             if (g, half) not in zag:
                 zag[g, half] = work.tile([P, 2, 256 * 4], BF16, name="zag", bufs=4, align_bytes=64)
-            words = za[:].rearrange("p u x -> p (u x)").bitcast(F32)
-            ps = psum.tile([P, 512], F32, name="zt_ps", tag="s2", bufs=3)
+            words = z_sb[:, g, t, :].bitcast(F32)
+            ps = psum.tile([P, 512], F32, name="zt_ps", tag=tag, bufs=bufs)
             for kg in range(2):
                 for u in range(2):
                     j = 2 * kg + u
                     nc.tensor.transpose(
-                        ps[:, j * P : (j + 1) * P],
-                        words[:, 256 * u + P * kg : 256 * u + P * (kg + 1)],
-                        ident[:],
+                        ps[:, j * P : (j + 1) * P], words[:, 256 * kg + u : 256 * (kg + 1) : 2], ident[:]
                     )
-            dst = zag[g, half][:].rearrange("p k x -> p (k x)").bitcast(F32).rearrange("p (k n u) -> p k n u", k=2, u=2)
-            copy(
-                out=dst[:, :, s * P : (s + 1) * P, :],
-                in_=ps[:].rearrange("p (k u n) -> p k n u", k=2, u=2),
-            )
+            return ps
+
+        def za_mul(g, t, ps):
+            half, s = divmod(t, 2)
+            for kg in range(2):
+                nc.vector.tensor_tensor(
+                    out=zag[g, half][:, kg, 512 * s : 512 * s + 512].rearrange("p (n u e) -> p n u e", u=2, e=2),
+                    in0=ps[:, 256 * kg : 256 * kg + 256].bitcast(BF16).rearrange("p (u n e) -> p n u e", u=2, e=2),
+                    in1=a_k[:, kg, :].rearrange("p (u e) -> p u e", u=2).unsqueeze(1).to_broadcast([P, P, 2, 2]),
+                    op=ALU.mult,
+                )
 
         def za_quant(g, half):
             for kg in range(2):
@@ -195,14 +176,14 @@ def tile_coupledlstmfoldedweightgradient_kernel(
             for kg in range(2):
                 nc.tensor.matmul_mx(
                     out=mm[:],
-                    lhsT=w_sb[:, kg, 2 * col : 2 * col + 256].bitcast(FP4X4),
+                    lhsT=w_sb[gate][:, kg, 2 * hc * P : 2 * hc * P + 256].bitcast(FP4X4),
                     lhsT_scale=wsc[:, kg, col : col + P],
                     rhs=zaq[g][:, kg, :].bitcast(FP8X4),
                     rhs_scale=zas[g][:, kg, :],
                     start=(kg == 0),
                     stop=(kg == 1),
                 )
-            act = work.tile([P, 512], F32, name="act%d" % gate, bufs=2, align_bytes=64)
+            act = work.tile([P, 512], F32, name="act%d" % gate, bufs=3, align_bytes=64)
             nc.scalar.activation(
                 out=act[:],
                 in_=mm[:],
@@ -215,6 +196,11 @@ def tile_coupledlstmfoldedweightgradient_kernel(
         def gates(i):
             for gate in (GG, GO, GF):
                 gate_mm(i, gate)
+
+        def square_g(i):
+            sq = work.tile([P, 512], F32, name="act3", bufs=3, align_bytes=64)
+            nc.scalar.activation(out=sq[:], in_=acts[i, GG][:], func=ACTF.Square, scale=ROOT2)
+            acts[i, GSQ] = sq
 
         def turn_gate(i, gate):
             tp = psum.tile([P, 512], F32, name="tp%d" % gate, tag="tp%d" % gate, bufs=1)
@@ -233,9 +219,6 @@ def tile_coupledlstmfoldedweightgradient_kernel(
 
         def ht(i, name):
             return vals[i, name][:].rearrange("p (h t) -> p h t", t=4)
-
-        def square_g(i):
-            nc.scalar.activation(out=new(i, "g2"), in_=turned[i, GG], func=ACTF.Square, scale=ROOT2)
 
         def phase_a(i):
             hc, g = divmod(i, 2)
@@ -283,13 +266,18 @@ def tile_coupledlstmfoldedweightgradient_kernel(
         def delta_g(i):
             dpg = work.tile([P, 512], BF16, name="dpg", bufs=2, align_bytes=64)
             nc.vector.scalar_tensor_tensor(
-                out=dpg[:], in0=vals[i, "g2"][:], scalar=2.0, in1=vals[i, "y"][:], op0=ALU.subtract, op1=ALU.mult
+                out=dpg[:].rearrange("p (h t) -> p h t", t=4),
+                in0=turned[i, GSQ],
+                scalar=2.0,
+                in1=ht(i, "y"),
+                op0=ALU.subtract,
+                op1=ALU.mult,
             )
             return dpg
 
         def delta_tiles(i):
-            codes = work.tile([P, 3 * P], U32, name="dq", bufs=4, align_bytes=64)
-            scales = work.tile([P, 3 * P], U8, name="dqs", bufs=4, align_bytes=64)
+            codes = work.tile([P, 3 * P], U32, name="dq", bufs=6, align_bytes=64)
+            scales = work.tile([P, 3 * P], U8, name="dqs", bufs=6, align_bytes=64)
             deltas[i] = (codes, scales)
 
         gp = {}
@@ -298,19 +286,22 @@ def tile_coupledlstmfoldedweightgradient_kernel(
             phase_y(i)
             dpf = delta_f(i, nc.gpsimd)
             gp[i] = (delta_o(i, nc.gpsimd), dpf)
+            for how, cast, plane in pending:
+                if how == "G":
+                    cast()
 
-        def phase_b(i, fill):
+        def phase_b(i, dpg, fill):
             delta_tiles(i)
             dpo, dpf = gp[i]
-            dpg = delta_g(i)
-            for cast, plane in fill:
-                cast()
+            for how, cast, plane in fill:
+                if how == "V":
+                    cast()
             delta_quant(i, GO, dpo)
             delta_quant(i, GF, dpf)
-            for cast, plane in fill[:1]:
+            for how, cast, plane in fill[:1]:
                 plane()
             delta_quant(i, GG, dpg)
-            for cast, plane in fill[1:]:
+            for how, cast, plane in fill[1:]:
                 plane()
 
         def phase_b_last(i):
@@ -334,9 +325,9 @@ def tile_coupledlstmfoldedweightgradient_kernel(
                 in_=ow[hc, G][:].bitcast(I32).rearrange("p (s m) -> p s m", s=3),
             )
 
-        def out_bank(hc, G, gate, how):
+        def out_bank(hc, G, gate, how, tag="s2", bufs=2):
             col = gate * HID + hc * P
-            mm = psum.tile([P, 512], F32, name="s2_ps", tag="s2", bufs=3)
+            mm = psum.tile([P, 512], F32, name="s2_ps", tag=tag, bufs=bufs)
             for t in range(4):
                 ch = slice(512 * G + P * t, 512 * G + P * t + P)
                 for g in range(2):
@@ -366,8 +357,13 @@ def tile_coupledlstmfoldedweightgradient_kernel(
             words = ow[hc, G]
 
             def cast():
+                res_v = res[:].rearrange("p (t m) -> p m t", t=4)
                 if how == "V":
-                    nc.vector.tensor_copy(out=og_v, in_=res[:].rearrange("p (t m) -> p m t", t=4))
+                    nc.vector.tensor_copy(out=og_v, in_=res_v)
+                if how == "G":
+                    nc.gpsimd.tensor_scalar(
+                        out=og_v, in0=res_v, scalar1=1.0, scalar2=1.0, op0=ALU.mult, op1=ALU.mult
+                    )
 
             def plane():
                 nc.vector.quantize_mx(
@@ -379,7 +375,7 @@ def tile_coupledlstmfoldedweightgradient_kernel(
                 if done[hc, G] == 3:
                     store_words(hc, G)
 
-            pending.append((cast, plane))
+            pending.append((how, cast, plane))
 
         def take_pending(n=99):
             got = list(pending[:n])
@@ -388,86 +384,100 @@ def tile_coupledlstmfoldedweightgradient_kernel(
             pending.extend(rest)
             return got
 
-        VC, AC = nc.vector.tensor_copy, nc.scalar.copy
         dhq = keep.tile([P, 2, 4, HID], BF16, name="dhq", align_bytes=64)
 
         def quarter_dh(g):
             nc.vector.tensor_scalar_mul(out=dhq[:, g], in0=dh_sb[:, g], scalar1=0.25)
 
-        tiles = [za_mul(0, t) for t in range(4)]
-        for t in range(4):
-            za_turn(0, t, tiles[t], VC if t == 2 else AC)
-        make_bias()
         nc.vector.tensor_copy(out=r_f[:], in_=r_t[:].rearrange("p g t -> p (g t)"))
-        za_quant(0, 0)
-        za_quant(0, 1)
-        gates(0)
-        zr00 = zr_mul(0, 0)
-        tiles = [za_mul(1, t) for t in range(4)]
-        turn(0)
-        square_g(0)
-        quarter_dh(0)
-        phase_a(0)
         for t in range(4):
-            za_turn(1, t, tiles[t], AC)
-        cell_tanh(0)
-        cell_square(0)
-        za_quant(1, 0)
-        zr_quant(0, 0, zr00)
-        za_quant(1, 1)
-        gates(1)
-        zr01 = zr_mul(0, 1)
-        turn(1)
-        square_g(1)
+            za_mul(0, t, za_turn(0, t, "s2", 2))
+            zr_scale(0, t)
+            if t % 2:
+                za_quant(0, t // 2)
+        make_bias()
+        U = [0, 2, 1, 3, 4, 5, 6, 7]
+        gates(U[0])
+        square_g(U[0])
+        turn(U[0])
+        gates(U[1])
+        square_g(U[1])
+        joins = [zr_join(0, 0), zr_join(0, 1)]
+        quarter_dh(0)
+        phase_a(U[0])
+        for t in range(4):
+            za_mul(1, t, za_turn(1, t, "s2", 2))
+            if t % 2:
+                za_quant(1, t // 2)
+        cell_tanh(U[0])
+        cell_square(U[0])
+        turn(U[1])
+        turn_gate(U[0], GSQ)
         zr_scale(1, 0)
-        quarter_dh(1)
+        gates(U[2])
+        square_g(U[2])
 
-        hows = "VVAVVA"
+        hows = "GAVVAV"
         for i in range(1, 8):
-            phase_y_and_gp(i - 1)
-            if i < 7:
-                gates(i + 1)
-            phase_a(i)
-            if i == 1:
-                zr_quant(0, 1, zr01)
-            if i == 2:
-                zr10 = zr_join(1, 0)
-                zr11 = zr_join(1, 1)
-            phase_b(i - 1, take_pending())
-            if i == 2:
-                zr_quant(1, 0, zr10)
-                zr_quant(1, 1, zr11)
             banks = []
             if i >= 3:
                 hc, G = divmod(i - 3, 2)
                 banks = [(hc, G, gate) for gate in (GO, GG, GF)]
             if i == 7:
                 banks += [(hc, 1, gate) for gate in (GO, GG, GF)]
-            if banks:
-                out_bank(*banks[0], hows[0])
-            cell_tanh(i)
-            cell_square(i)
-            if i < 7:
-                turn(i + 1)
-                square_g(i + 1)
+            nxt = U[i + 2] if i + 2 < 8 else None
+            phase_y_and_gp(U[i - 1])
+            phase_a(U[i])
+            dpg = delta_g(U[i - 1])
             if i == 1:
-                for t in range(1, 4):
-                    zr_scale(1, t)
-            for k in range(1, len(banks)):
+                quarter_dh(1)
+                zr_quant(0, 0, joins[0])
+                zr_quant(0, 1, joins[1])
+            if i == 3:
+                joins = [zr_join(1, 0), zr_join(1, 1)]
+            phase_b(U[i - 1], dpg, take_pending())
+            if i == 3:
+                zr_quant(1, 0, joins[0])
+                zr_quant(1, 1, joins[1])
+            if nxt:
+                gate_mm(nxt, GG)
+            if i >= 4:
+                out_bank(*banks[0], hows[0])
+            cell_tanh(U[i])
+            cell_square(U[i])
+            if nxt:
+                gate_mm(nxt, GO)
+            if i >= 4:
+                out_bank(*banks[1], hows[1])
+            if i < 7:
+                turn(U[i + 1])
+            turn_gate(U[i], GSQ)
+            if nxt:
+                gate_mm(nxt, GF)
+                square_g(nxt)
+            if i == 1:
+                zr_scale(1, 1)
+                zr_scale(1, 2)
+            if i == 2:
+                zr_scale(1, 3)
+            for k in range(2 if i >= 4 else 0, len(banks)):
                 out_bank(*banks[k], hows[k])
-        fill = take_pending()
-        for cast, plane in fill:
-            cast()
         phase_b_last(7)
-        for cast, plane in fill:
+        fill = take_pending()
+        for how, cast, plane in fill:
+            if how != "A":
+                cast()
+        for how, cast, plane in fill:
             plane()
+        spare = [("s2", 2), ("s2", 2), ("tp0", 1), ("tp1", 1), ("tp2", 1), ("s1", 2)]
         for gate in (GO, GG, GF):
             for G in range(2):
-                out_bank(3, G, gate, "V" if G else "A")
+                out_bank(3, G, gate, "V" if G else "A", *spare.pop(0))
             fill = take_pending()
-            for cast, plane in fill:
-                cast()
-            for cast, plane in fill:
+            for how, cast, plane in fill:
+                if how == "V":
+                    cast()
+            for how, cast, plane in fill:
                 plane()
         for q in range(4):
             nc.sync.dma_start(

@@ -131,28 +131,40 @@ def tile_coupledlstmfoldedweightgradient_kernel(
                     out=zaq[g][:, kg, cols].bitcast(FP8X4), scales=zas[g][:, kg, cols], in_=zag[g, half][:, kg, :]
                 )
 
-        def zr_scale(g, t):
+        def za_quant_slice(g, t):
+            half, s = divmod(t, 2)
+            for kg in range(2):
+                cols = slice(P * t, P * t + P)
+                nc.vector.quantize_mx(
+                    out=zaq[g][:, kg, cols].bitcast(FP8X4),
+                    scales=zas[g][:, kg, cols],
+                    in_=zag[g, half][:, kg, 512 * s : 512 * s + 512],
+                )
+
+        def zr_scale(g, t, G0=0):
             if g not in zrn:
                 zrn[g] = work.tile([P, 4, CH], BF16, name="zrn", bufs=1, align_bytes=64)
             nc.scalar.activation(
-                out=zrn[g][:, t, :].rearrange("p (k s m) -> p k s m", k=2, s=4),
-                in_=z_sb[:, g, t, :].rearrange("p (k m s) -> p k s m", k=2, s=4),
+                out=zrn[g][:, t, 512 * G0 :].rearrange("p (k s m) -> p k s m", k=2 - G0, s=4),
+                in_=z_sb[:, g, t, 512 * G0 :].rearrange("p (k m s) -> p k s m", k=2 - G0, s=4),
                 func=ACTF.Copy,
                 scale=r_f[:, 4 * g + t : 4 * g + t + 1],
             )
 
-        def zr_mul(g, G):
-            zr = work.tile([P, 512 * 4], BF16, name="zr", bufs=2, align_bytes=64)
-            nc.vector.tensor_tensor(
-                out=zr[:].rearrange("p (s m t) -> p s m t", s=4, t=4),
-                in0=z_sb[:, g, :, 512 * G : 512 * G + 512].rearrange("p t (m s) -> p s m t", s=4),
-                in1=r_t[:, g, :].unsqueeze(1).unsqueeze(1).to_broadcast([P, 4, P, 4]),
-                op=ALU.mult,
-            )
+        def zr_new():
+            zr = work.tile([P, 512 * 4], BF16, name="zr", bufs=3, align_bytes=64)
             return zr
 
+        def zr_mul_piece(g, G, s, zr):
+            nc.gpsimd.tensor_tensor(
+                out=zr[:, 512 * s : 512 * s + 512].rearrange("p (m t) -> p m t", t=4),
+                in0=z_sb[:, g, :, 512 * G : 512 * G + 512].rearrange("p t (m s) -> p s m t", s=4)[:, s],
+                in1=r_t[:, g, :].unsqueeze(1).to_broadcast([P, P, 4]),
+                op=ALU.mult,
+            )
+
         def zr_join(g, G):
-            zr = work.tile([P, 512 * 4], BF16, name="zr", bufs=2, align_bytes=64)
+            zr = zr_new()
             nc.vector.tensor_copy(
                 out=zr[:].rearrange("p (c t) -> p c t", t=4),
                 in_=zrn[g][:, :, 512 * G : 512 * G + 512].rearrange("p t c -> p c t"),
@@ -169,20 +181,31 @@ def tile_coupledlstmfoldedweightgradient_kernel(
         deltas = {}
         marks = {}
 
-        def gate_mm(i, gate):
+        def gate_pass(mm, i, gate, cols):
             hc, g = divmod(i, 2)
             col = gate * HID + hc * P
-            mm = psum.tile([P, 512], F32, name="s1_ps", tag="s1", bufs=2)
             for kg in range(2):
                 nc.tensor.matmul_mx(
-                    out=mm[:],
+                    out=mm[:, cols],
                     lhsT=w_sb[gate][:, kg, 2 * hc * P : 2 * hc * P + 256].bitcast(FP4X4),
                     lhsT_scale=wsc[:, kg, col : col + P],
-                    rhs=zaq[g][:, kg, :].bitcast(FP8X4),
-                    rhs_scale=zas[g][:, kg, :],
+                    rhs=zaq[g][:, kg, cols].bitcast(FP8X4),
+                    rhs_scale=zas[g][:, kg, cols],
                     start=(kg == 0),
                     stop=(kg == 1),
                 )
+
+        def gate_bank():
+            mm = psum.tile([P, 512], F32, name="s1_ps", tag="s1", bufs=2)
+            return mm
+
+        def gate_mm(i, gate):
+            mm = gate_bank()
+            gate_pass(mm, i, gate, slice(0, 512))
+            gate_act(i, gate, mm)
+
+        def gate_act(i, gate, mm):
+            hc = i // 2
             act = work.tile([P, 512], F32, name="act%d" % gate, bufs=3, align_bytes=64)
             nc.scalar.activation(
                 out=act[:],
@@ -242,10 +265,10 @@ def tile_coupledlstmfoldedweightgradient_kernel(
             new(i, "sq")
             nc.scalar.activation(out=vals[i, "sq"][:], in_=vals[i, "tc"][:], func=ACTF.Square, scale=ROOT_HALF)
 
-        def delta_quant(i, gate, src):
+        def delta_quant(i, first, n, src):
             codes, scales = deltas[i]
-            cols = slice(gate * P, gate * P + P)
-            nc.vector.quantize_mx(out=codes[:, cols].bitcast(FP8X4), scales=scales[:, cols], in_=src[:])
+            cols = slice(first * P, (first + n) * P)
+            nc.vector.quantize_mx(out=codes[:, cols].bitcast(FP8X4), scales=scales[:, cols], in_=src)
 
         def phase_y(i):
             new(i, "y")
@@ -253,15 +276,15 @@ def tile_coupledlstmfoldedweightgradient_kernel(
                 out=vals[i, "y"][:], in0=vals[i, "sq"][:], scalar=0.5, in1=vals[i, "e"][:], op0=ALU.subtract, op1=ALU.mult
             )
 
+        def delta_pair(i):
+            pair = work.tile([P, 2, 512], BF16, name="dpof", bufs=2, align_bytes=64)
+            vals[i, "of"] = pair
+
         def delta_o(i, eng):
-            dpo = work.tile([P, 512], BF16, name="dpo", bufs=2, align_bytes=64)
-            eng.tensor_tensor(out=dpo[:], in0=vals[i, "t1"][:], in1=vals[i, "tc"][:], op=ALU.mult)
-            return dpo
+            eng.tensor_tensor(out=vals[i, "of"][:, 0, :], in0=vals[i, "t1"][:], in1=vals[i, "tc"][:], op=ALU.mult)
 
         def delta_f(i, eng):
-            dpf = work.tile([P, 512], BF16, name="dpf", bufs=2, align_bytes=64)
-            eng.tensor_tensor(out=dpf[:], in0=vals[i, "y"][:], in1=vals[i, "w"][:], op=ALU.mult)
-            return dpf
+            eng.tensor_tensor(out=vals[i, "of"][:, 1, :], in0=vals[i, "y"][:], in1=vals[i, "w"][:], op=ALU.mult)
 
         def delta_g(i):
             dpg = work.tile([P, 512], BF16, name="dpg", bufs=2, align_bytes=64)
@@ -280,39 +303,37 @@ def tile_coupledlstmfoldedweightgradient_kernel(
             scales = work.tile([P, 3 * P], U8, name="dqs", bufs=6, align_bytes=64)
             deltas[i] = (codes, scales)
 
-        gp = {}
-
         def phase_y_and_gp(i):
             phase_y(i)
-            dpf = delta_f(i, nc.gpsimd)
-            gp[i] = (delta_o(i, nc.gpsimd), dpf)
+            delta_pair(i)
+            delta_f(i, nc.gpsimd)
+            delta_o(i, nc.gpsimd)
             for how, cast, plane in pending:
                 if how == "G":
                     cast()
 
         def phase_b(i, dpg, fill):
             delta_tiles(i)
-            dpo, dpf = gp[i]
             for how, cast, plane in fill:
                 if how == "V":
                     cast()
-            delta_quant(i, GO, dpo)
-            delta_quant(i, GF, dpf)
+            delta_quant(i, 0, 2, vals[i, "of"][:].rearrange("p s x -> p (s x)"))
             for how, cast, plane in fill[:1]:
                 plane()
-            delta_quant(i, GG, dpg)
+            delta_quant(i, 2, 1, dpg[:])
             for how, cast, plane in fill[1:]:
                 plane()
 
         def phase_b_last(i):
             delta_tiles(i)
-            dpo = delta_o(i, nc.vector)
+            delta_pair(i)
+            delta_o(i, nc.vector)
             phase_y(i)
-            delta_quant(i, GO, dpo)
+            delta_quant(i, 0, 1, vals[i, "of"][:, 0, :])
             dpg = delta_g(i)
-            dpf = delta_f(i, nc.vector)
-            delta_quant(i, GG, dpg)
-            delta_quant(i, GF, dpf)
+            delta_f(i, nc.vector)
+            delta_quant(i, 2, 1, dpg[:])
+            delta_quant(i, 1, 1, vals[i, "of"][:, 1, :])
 
         ow = {}
         done = {}
@@ -325,8 +346,10 @@ def tile_coupledlstmfoldedweightgradient_kernel(
                 in_=ow[hc, G][:].bitcast(I32).rearrange("p (s m) -> p s m", s=3),
             )
 
-        def out_bank(hc, G, gate, how, tag="s2", bufs=2):
+        def out_bank(hc, G, gate, how, tag="s2", bufs=2, copy=nc.scalar.copy):
             col = gate * HID + hc * P
+            slot = {GO: 0, GF: 1, GG: 2}[gate]
+            dcol = slice(slot * P, slot * P + P)
             mm = psum.tile([P, 512], F32, name="s2_ps", tag=tag, bufs=bufs)
             for t in range(4):
                 ch = slice(512 * G + P * t, 512 * G + P * t + P)
@@ -336,13 +359,13 @@ def tile_coupledlstmfoldedweightgradient_kernel(
                         out=mm[:, P * t : P * t + P],
                         lhsT=zrq[g][:, ch].bitcast(FP8X4),
                         lhsT_scale=zrs[g][:, ch],
-                        rhs=codes[:, gate * P : gate * P + P].bitcast(FP8X4),
-                        rhs_scale=scales[:, gate * P : gate * P + P],
+                        rhs=codes[:, dcol].bitcast(FP8X4),
+                        rhs_scale=scales[:, dcol],
                         start=(g == 0),
                         stop=(g == 1),
                     )
             res = work.tile([P, 512], F32, name="res", bufs=6, align_bytes=64)
-            nc.scalar.copy(out=res[:], in_=mm[:])
+            copy(out=res[:], in_=mm[:])
             nc.sync.dma_start(
                 out=out_0[512 * G : 512 * G + 512, col : col + P].rearrange("(p t) m -> p t m", t=4),
                 in_=res[:].rearrange("p (t m) -> p t m", t=4),
@@ -389,22 +412,31 @@ def tile_coupledlstmfoldedweightgradient_kernel(
         def quarter_dh(g):
             nc.vector.tensor_scalar_mul(out=dhq[:, g], in0=dh_sb[:, g], scalar1=0.25)
 
-        nc.vector.tensor_copy(out=r_f[:], in_=r_t[:].rearrange("p g t -> p (g t)"))
-        for t in range(4):
-            za_mul(0, t, za_turn(0, t, "s2", 2))
-            zr_scale(0, t)
-            if t % 2:
-                za_quant(0, t // 2)
-        make_bias()
+        nc.scalar.copy(out=r_f[:], in_=r_t[:].rearrange("p g t -> p (g t)"))
         U = [0, 2, 1, 3, 4, 5, 6, 7]
-        gates(U[0])
+        first = {GG: gate_bank(), GO: gate_bank(), GF: psum.tile([P, 512], F32, name="first_f", tag="tp3", bufs=1)}
+        slots = [("s2", 2), ("s2", 2), ("tp0", 1), ("tp1", 1)]
+        banks = [za_turn(0, t, *slots[t]) for t in range(4)]
+        for t in range(4):
+            za_mul(0, t, banks[t])
+            zr_scale(0, t)
+            za_quant_slice(0, t)
+        make_bias()
+        for t in range(4):
+            for gate in (GG, GO, GF):
+                gate_pass(first[gate], U[0], gate, slice(P * t, P * t + P))
+        for gate in (GG, GO, GF):
+            gate_act(U[0], gate, first[gate])
         square_g(U[0])
         turn(U[0])
         gates(U[1])
         square_g(U[1])
         joins = [zr_join(0, 0), zr_join(0, 1)]
         quarter_dh(0)
+        zr_quant(0, 0, joins[0])
         phase_a(U[0])
+        zr10 = zr_new()
+        zr_mul_piece(1, 0, 0, zr10)
         for t in range(4):
             za_mul(1, t, za_turn(1, t, "s2", 2))
             if t % 2:
@@ -413,38 +445,37 @@ def tile_coupledlstmfoldedweightgradient_kernel(
         cell_square(U[0])
         turn(U[1])
         turn_gate(U[0], GSQ)
-        zr_scale(1, 0)
+        nc.scalar.activation(out=dhq[:, 1], in_=dh_sb[:, 1], func=ACTF.Copy, scale=0.25)
         gates(U[2])
         square_g(U[2])
 
-        hows = "GAVVAV"
+        hows = "GAVAAA"
+        BANKS = [(hc, G, gate) for hc in range(3) for G in range(2) for gate in (GO, GG, GF)]
+        SPLIT = (0, 0, 0, 0, 2, 6, 10, 14, 18)
         for i in range(1, 8):
-            banks = []
-            if i >= 3:
-                hc, G = divmod(i - 3, 2)
-                banks = [(hc, G, gate) for gate in (GO, GG, GF)]
-            if i == 7:
-                banks += [(hc, 1, gate) for gate in (GO, GG, GF)]
+            banks = BANKS[SPLIT[i] : SPLIT[i + 1]]
             nxt = U[i + 2] if i + 2 < 8 else None
             phase_y_and_gp(U[i - 1])
             phase_a(U[i])
             dpg = delta_g(U[i - 1])
             if i == 1:
-                quarter_dh(1)
-                zr_quant(0, 0, joins[0])
                 zr_quant(0, 1, joins[1])
+            if i < 4:
+                zr_mul_piece(1, 0, i, zr10)
             if i == 3:
-                joins = [zr_join(1, 0), zr_join(1, 1)]
+                zr11 = zr_join(1, 1)
             phase_b(U[i - 1], dpg, take_pending())
             if i == 3:
-                zr_quant(1, 0, joins[0])
-                zr_quant(1, 1, joins[1])
-            if nxt:
+                zr_quant(1, 0, zr10)
+                zr_quant(1, 1, zr11)
+            if nxt and i > 2:
                 gate_mm(nxt, GG)
             if i >= 4:
                 out_bank(*banks[0], hows[0])
             cell_tanh(U[i])
             cell_square(U[i])
+            if nxt and i <= 2:
+                gate_mm(nxt, GG)
             if nxt:
                 gate_mm(nxt, GO)
             if i >= 4:
@@ -455,30 +486,35 @@ def tile_coupledlstmfoldedweightgradient_kernel(
             if nxt:
                 gate_mm(nxt, GF)
                 square_g(nxt)
-            if i == 1:
-                zr_scale(1, 1)
-                zr_scale(1, 2)
-            if i == 2:
-                zr_scale(1, 3)
+            if i in (1, 2):
+                zr_scale(1, 2 * i - 2, 1)
+                zr_scale(1, 2 * i - 1, 1)
             for k in range(2 if i >= 4 else 0, len(banks)):
                 out_bank(*banks[k], hows[k])
         phase_b_last(7)
         fill = take_pending()
-        for how, cast, plane in fill:
-            if how != "A":
-                cast()
-        for how, cast, plane in fill:
-            plane()
-        spare = [("s2", 2), ("s2", 2), ("tp0", 1), ("tp1", 1), ("tp2", 1), ("s1", 2)]
-        for gate in (GO, GG, GF):
-            for G in range(2):
-                out_bank(3, G, gate, "V" if G else "A", *spare.pop(0))
-            fill = take_pending()
-            for how, cast, plane in fill:
-                if how == "V":
+        spare = {
+            (GO, 0): ("s2", 2),
+            (GO, 1): ("s2", 2),
+            (GG, 0): ("tp0", 1),
+            (GG, 1): ("tp1", 1),
+            (GF, 0): ("tp2", 1),
+            (GF, 1): ("s1", 2),
+        }
+
+        def finish(batch):
+            for how, cast, plane in batch:
+                if how != "A":
                     cast()
-            for how, cast, plane in fill:
+            for how, cast, plane in batch:
                 plane()
+
+        for gate in (GO, GG, GF):
+            out_bank(3, 0, gate, "A", *spare[gate, 0])
+            out_bank(3, 1, gate, "V", *spare[gate, 1], nc.vector.tensor_copy)
+            if gate == GO:
+                finish(fill)
+            finish(take_pending())
         for q in range(4):
             nc.sync.dma_start(
                 out=out_2[:, 4 * q : 4 * q + 4, :].rearrange("g r m -> r g m").bitcast(I32),

import math
from contextlib import ExitStack

import concourse.mybir as mybir
from concourse.masks import make_identity

TOK, CH, HID = 1024, 1024, 512
GATES = 3 * HID
P = 128
FLOPS = 2 * 2 * TOK * CH * GATES

F32 = mybir.dt.float32
BF16 = mybir.dt.bfloat16
U32 = mybir.dt.uint32
I32 = mybir.dt.int32
U8 = mybir.dt.uint8
FP8X4 = mybir.dt.float8_e4m3fn_x4
FP4X4 = mybir.dt.float4_e2m1fn_x4
ACTF = mybir.ActivationFunctionType
ALU = mybir.AluOpType

ROOT2 = math.sqrt(2.0)
ROOT_HALF = math.sqrt(0.5)

GF, GG, GO, GSQ = 0, 1, 2, 3
GATE_SCALE = {GF: -0.5, GG: 1.0, GO: 0.5}


def tile_coupledlstmfoldedweightgradient_kernel(
    tc, z, c, w_words, w_scales, b, a, r, dh_new, out_0, out_1, out_2
):
    nc = tc.nc
    with ExitStack() as ctx:
        keep = ctx.enter_context(tc.tile_pool(name="keep", bufs=1))
        work = ctx.enter_context(tc.tile_pool(name="work", bufs=2))
        psum = ctx.enter_context(tc.psum_pool(name="psum", bufs=1))
        ctx.enter_context(tc.manual_schedule())

        warm = keep.tile([P, 1], F32, name="warm")
        nc.vector.memset(warm[:], 0.0)
        warm2 = keep.tile([P, 1], F32, name="warm2")
        nc.scalar.activation(out=warm2[:], in_=warm[:], func=ACTF.Tanh)
        ident = keep.tile([P, P], F32, name="ident", align_bytes=64)
        make_identity(nc, ident[:])

        a_k = keep.tile([P, 2, 4], BF16, name="a_k", align_bytes=64)
        nc.scalar.dma_start(out=a_k[:], in_=a.rearrange("(k p t) -> p k t", k=2, t=4))
        r_t = keep.tile([P, 2, 4], BF16, name="r_t", align_bytes=64)
        nc.scalar.dma_start(out=r_t[:], in_=r.rearrange("(g p t) -> p g t", g=2, t=4))
        z_sb = keep.tile([P, 2, 4, CH], BF16, name="z_sb", align_bytes=64)
        z_v = z.rearrange("(g p t) k -> g p t k", g=2, t=4)
        for t in range(4):
            nc.sync.dma_start(out=z_sb[:, 0, t, :], in_=z_v[0, :, t, :])
        b_row = keep.tile([P, P], BF16, name="b_row", align_bytes=64)
        nc.vector.memset(b_row[:], 0.0)
        nc.scalar.dma_start(out=b_row[0:12, :], in_=b.rearrange("(c h) -> c h", c=12))
        wsc = keep.tile([P, 2, GATES], U8, name="wsc", align_bytes=64)
        nc.vector.memset(wsc[:].rearrange("p k n -> p (k n)").bitcast(I32), 0)
        for q in range(4):
            nc.scalar.dma_start(
                out=wsc[32 * q : 32 * q + 4, :, :].bitcast(I32),
                in_=w_scales[:, 4 * q : 4 * q + 4, :].rearrange("k r n -> r k n").bitcast(I32),
            )
        w_sb = {}
        for gate in (GG, GO, GF):
            w_sb[gate] = keep.tile([P, 2, 2 * HID], U8, name="w_sb%d" % gate, align_bytes=64)
            nc.sync.dma_start(
                out=w_sb[gate][:].bitcast(I32),
                in_=w_words[:, :, 2 * gate * HID : 2 * (gate + 1) * HID].rearrange("k p n -> p k n").bitcast(I32),
            )
        c_sb = keep.tile([P, 2, 4, HID], BF16, name="c_sb", align_bytes=64)
        dh_sb = keep.tile([P, 2, 4, HID], BF16, name="dh_sb", align_bytes=64)
        c_v = c.rearrange("(g p t) h -> g p t h", g=2, t=4)
        dh_v = dh_new.rearrange("(g p t) h -> g p t h", g=2, t=4)
        nc.sync.dma_start(out=c_sb[:, 0], in_=c_v[0])
        nc.sync.dma_start(out=dh_sb[:, 0], in_=dh_v[0])
        for t in range(4):
            nc.sync.dma_start(out=z_sb[:, 1, t, :], in_=z_v[1, :, t, :])
        nc.sync.dma_start(out=c_sb[:, 1], in_=c_v[1])
        nc.sync.dma_start(out=dh_sb[:, 1], in_=dh_v[1])

        ident_b = keep.tile([P, P], BF16, name="ident_b", align_bytes=64)
        nc.vector.tensor_copy(out=ident_b[:], in_=ident[:])

        bias = keep.tile([P, 12], F32, name="bias")

        def make_bias():
            b_ps = psum.tile([P, P], BF16, name="b_ps", tag="s2", bufs=2)
            nc.tensor.transpose(b_ps[:], b_row[:], ident_b[:])
            for gate in (GF, GG, GO):
                cols = slice(4 * gate, 4 * gate + 4)
                nc.vector.tensor_scalar_mul(out=bias[:, cols], in0=b_ps[:, cols], scalar1=GATE_SCALE[gate])

        zaq = [keep.tile([P, 2, 512], U32, name="zaq%d" % g, align_bytes=64) for g in range(2)]
        zas = [keep.tile([P, 2, 512], U8, name="zas%d" % g, align_bytes=64) for g in range(2)]
        zrq = [keep.tile([P, CH], U32, name="zrq%d" % g, align_bytes=64) for g in range(2)]
        zrs = [keep.tile([P, CH], U8, name="zrs%d" % g, align_bytes=64) for g in range(2)]
        osc = keep.tile([P, 2, GATES], U8, name="osc", align_bytes=64)
        r_f = keep.tile([P, 8], F32, name="r_f")
        zag = {}
        zrn = {}

        def za_turn(g, t, tag, bufs):
            half, s = divmod(t, 2)
            if (g, half) not in zag:
                zag[g, half] = work.tile([P, 2, 256 * 4], BF16, name="zag", bufs=4, align_bytes=64)
            words = z_sb[:, g, t, :].bitcast(F32)
            ps = psum.tile([P, 512], F32, name="zt_ps", tag=tag, bufs=bufs)
            for kg in range(2):
                for u in range(2):
                    j = 2 * kg + u
                    nc.tensor.transpose(
                        ps[:, j * P : (j + 1) * P], words[:, 256 * kg + u : 256 * (kg + 1) : 2], ident[:]
                    )
            return ps

        def za_mul(g, t, ps):
            half, s = divmod(t, 2)
            for kg in range(2):
                nc.vector.tensor_tensor(
                    out=zag[g, half][:, kg, 512 * s : 512 * s + 512].rearrange("p (n u e) -> p n u e", u=2, e=2),
                    in0=ps[:, 256 * kg : 256 * kg + 256].bitcast(BF16).rearrange("p (u n e) -> p n u e", u=2, e=2),
                    in1=a_k[:, kg, :].rearrange("p (u e) -> p u e", u=2).unsqueeze(1).to_broadcast([P, P, 2, 2]),
                    op=ALU.mult,
                )

        def za_quant(g, half):
            for kg in range(2):
                cols = slice(256 * half, 256 * half + 256)
                nc.vector.quantize_mx(
                    out=zaq[g][:, kg, cols].bitcast(FP8X4), scales=zas[g][:, kg, cols], in_=zag[g, half][:, kg, :]
                )

        def za_quant_slice(g, t):
            half, s = divmod(t, 2)
            for kg in range(2):
                cols = slice(P * t, P * t + P)
                nc.vector.quantize_mx(
                    out=zaq[g][:, kg, cols].bitcast(FP8X4),
                    scales=zas[g][:, kg, cols],
                    in_=zag[g, half][:, kg, 512 * s : 512 * s + 512],
                )

        def zr_scale(g, t, G0=0):
            if g not in zrn:
                zrn[g] = work.tile([P, 4, CH], BF16, name="zrn", bufs=1, align_bytes=64)
            nc.scalar.activation(
                out=zrn[g][:, t, 512 * G0 :].rearrange("p (k s m) -> p k s m", k=2 - G0, s=4),
                in_=z_sb[:, g, t, 512 * G0 :].rearrange("p (k m s) -> p k s m", k=2 - G0, s=4),
                func=ACTF.Copy,
                scale=r_f[:, 4 * g + t : 4 * g + t + 1],
            )

        def zr_new():
            zr = work.tile([P, 512 * 4], BF16, name="zr", bufs=3, align_bytes=64)
            return zr

        def zr_mul_piece(g, G, s, zr):
            nc.gpsimd.tensor_tensor(
                out=zr[:, 512 * s : 512 * s + 512].rearrange("p (m t) -> p m t", t=4),
                in0=z_sb[:, g, :, 512 * G : 512 * G + 512].rearrange("p t (m s) -> p s m t", s=4)[:, s],
                in1=r_t[:, g, :].unsqueeze(1).to_broadcast([P, P, 4]),
                op=ALU.mult,
            )

        def zr_join(g, G):
            zr = zr_new()
            nc.vector.tensor_copy(
                out=zr[:].rearrange("p (c t) -> p c t", t=4),
                in_=zrn[g][:, :, 512 * G : 512 * G + 512].rearrange("p t c -> p c t"),
            )
            return zr

        def zr_quant(g, G, zr):
            cols = slice(512 * G, 512 * G + 512)
            nc.vector.quantize_mx(out=zrq[g][:, cols].bitcast(FP8X4), scales=zrs[g][:, cols], in_=zr[:])

        acts = {}
        turned = {}
        vals = {}
        deltas = {}
        marks = {}

        def gate_pass(mm, i, gate, cols):
            hc, g = divmod(i, 2)
            col = gate * HID + hc * P
            for kg in range(2):
                nc.tensor.matmul_mx(
                    out=mm[:, cols],
                    lhsT=w_sb[gate][:, kg, 2 * hc * P : 2 * hc * P + 256].bitcast(FP4X4),
                    lhsT_scale=wsc[:, kg, col : col + P],
                    rhs=zaq[g][:, kg, cols].bitcast(FP8X4),
                    rhs_scale=zas[g][:, kg, cols],
                    start=(kg == 0),
                    stop=(kg == 1),
                )

        def gate_bank():
            mm = psum.tile([P, 512], F32, name="s1_ps", tag="s1", bufs=2)
            return mm

        def gate_mm(i, gate):
            mm = gate_bank()
            gate_pass(mm, i, gate, slice(0, 512))
            gate_act(i, gate, mm)

        def gate_act(i, gate, mm):
            hc = i // 2
            act = work.tile([P, 512], F32, name="act%d" % gate, bufs=3, align_bytes=64)
            nc.scalar.activation(
                out=act[:],
                in_=mm[:],
                func=ACTF.Tanh,
                bias=bias[:, 4 * gate + hc : 4 * gate + hc + 1],
                scale=GATE_SCALE[gate],
            )
            acts[i, gate] = act

        def gates(i):
            for gate in (GG, GO, GF):
                gate_mm(i, gate)

        def square_g(i):
            sq = work.tile([P, 512], F32, name="act3", bufs=3, align_bytes=64)
            nc.scalar.activation(out=sq[:], in_=acts[i, GG][:], func=ACTF.Square, scale=ROOT2)
            acts[i, GSQ] = sq

        def turn_gate(i, gate):
            tp = psum.tile([P, 512], F32, name="tp%d" % gate, tag="tp%d" % gate, bufs=1)
            for t in range(4):
                nc.tensor.transpose(tp[:, t * P : (t + 1) * P], acts[i, gate][:, t * P : (t + 1) * P], ident[:])
            turned[i, gate] = tp[:].rearrange("p (t h) -> p h t", t=4)

        def turn(i):
            for gate in (GG, GO, GF):
                turn_gate(i, gate)

        def new(i, name):
            v = work.tile([P, 512], F32, name=name, bufs=2, align_bytes=64)
            vals[i, name] = v
            return v[:].rearrange("p (h t) -> p h t", t=4)

        def ht(i, name):
            return vals[i, name][:].rearrange("p (h t) -> p h t", t=4)

        def phase_a(i):
            hc, g = divmod(i, 2)
            cols = slice(hc * P, hc * P + P)
            c_ht = c_sb[:, g, :, cols].rearrange("p t h -> p h t")
            dh_ht = dhq[:, g, :, cols].rearrange("p t h -> p h t")
            f_, g_, o_ = turned[i, GF], turned[i, GG], turned[i, GO]
            stt = nc.vector.scalar_tensor_tensor
            nc.vector.tensor_tensor(out=new(i, "d"), in0=c_ht, in1=g_, op=ALU.subtract)
            stt(out=new(i, "do"), in0=o_, scalar=1.0, in1=dh_ht, op0=ALU.add, op1=ALU.mult)
            stt(out=new(i, "w"), in0=f_, scalar=1.0, in1=ht(i, "d"), op0=ALU.subtract, op1=ALU.mult)
            stt(out=new(i, "t1"), in0=o_, scalar=1.0, in1=ht(i, "do"), op0=ALU.subtract, op1=ALU.mult)
            stt(out=new(i, "s"), in0=ht(i, "w"), scalar=0.5, in1=g_, op0=ALU.mult, op1=ALU.subtract)
            stt(out=new(i, "e"), in0=f_, scalar=1.0, in1=ht(i, "do"), op0=ALU.add, op1=ALU.mult)

        def cell_tanh(i):
            new(i, "tc")
            nc.scalar.activation(out=vals[i, "tc"][:], in_=vals[i, "s"][:], func=ACTF.Tanh)

        def cell_square(i):
            new(i, "sq")
            nc.scalar.activation(out=vals[i, "sq"][:], in_=vals[i, "tc"][:], func=ACTF.Square, scale=ROOT_HALF)

        def delta_quant(i, first, n, src):
            codes, scales = deltas[i]
            cols = slice(first * P, (first + n) * P)
            nc.vector.quantize_mx(out=codes[:, cols].bitcast(FP8X4), scales=scales[:, cols], in_=src)

        def phase_y(i):
            new(i, "y")
            nc.vector.scalar_tensor_tensor(
                out=vals[i, "y"][:], in0=vals[i, "sq"][:], scalar=0.5, in1=vals[i, "e"][:], op0=ALU.subtract, op1=ALU.mult
            )

        def delta_pair(i):
            pair = work.tile([P, 2, 512], BF16, name="dpof", bufs=2, align_bytes=64)
            vals[i, "of"] = pair

        def delta_o(i, eng):
            eng.tensor_tensor(out=vals[i, "of"][:, 0, :], in0=vals[i, "t1"][:], in1=vals[i, "tc"][:], op=ALU.mult)

        def delta_f(i, eng):
            eng.tensor_tensor(out=vals[i, "of"][:, 1, :], in0=vals[i, "y"][:], in1=vals[i, "w"][:], op=ALU.mult)

        def delta_g(i):
            dpg = work.tile([P, 512], BF16, name="dpg", bufs=2, align_bytes=64)
            nc.vector.scalar_tensor_tensor(
                out=dpg[:].rearrange("p (h t) -> p h t", t=4),
                in0=turned[i, GSQ],
                scalar=2.0,
                in1=ht(i, "y"),
                op0=ALU.subtract,
                op1=ALU.mult,
            )
            return dpg

        def delta_tiles(i):
            codes = work.tile([P, 3 * P], U32, name="dq", bufs=6, align_bytes=64)
            scales = work.tile([P, 3 * P], U8, name="dqs", bufs=6, align_bytes=64)
            deltas[i] = (codes, scales)

        def phase_y_and_gp(i):
            phase_y(i)
            delta_pair(i)
            delta_f(i, nc.gpsimd)
            delta_o(i, nc.gpsimd)
            for how, cast, plane in pending:
                if how == "G":
                    cast()

        def phase_b(i, dpg, fill):
            delta_tiles(i)
            for how, cast, plane in fill:
                if how == "V":
                    cast()
            delta_quant(i, 0, 2, vals[i, "of"][:].rearrange("p s x -> p (s x)"))
            for how, cast, plane in fill[:1]:
                plane()
            delta_quant(i, 2, 1, dpg[:])
            for how, cast, plane in fill[1:]:
                plane()

        def phase_b_last(i):
            delta_tiles(i)
            delta_pair(i)
            delta_o(i, nc.vector)
            phase_y(i)
            delta_quant(i, 0, 1, vals[i, "of"][:, 0, :])
            dpg = delta_g(i)
            delta_f(i, nc.vector)
            delta_quant(i, 2, 1, dpg[:])
            delta_quant(i, 1, 1, vals[i, "of"][:, 1, :])

        ow = {}
        done = {}
        pending = []

        def store_words(hc, G):
            dst = out_1[G].rearrange("p m b -> p (m b)").bitcast(I32).rearrange("p (s m) -> p s m", s=3)
            nc.sync.dma_start(
                out=dst[:, :, hc * P : hc * P + P],
                in_=ow[hc, G][:].bitcast(I32).rearrange("p (s m) -> p s m", s=3),
            )

        def out_bank(hc, G, gate, how, tag="s2", bufs=2, copy=nc.scalar.copy):
            col = gate * HID + hc * P
            slot = {GO: 0, GF: 1, GG: 2}[gate]
            dcol = slice(slot * P, slot * P + P)
            mm = psum.tile([P, 512], F32, name="s2_ps", tag=tag, bufs=bufs)
            for t in range(4):
                ch = slice(512 * G + P * t, 512 * G + P * t + P)
                for g in range(2):
                    codes, scales = deltas[2 * hc + g]
                    nc.tensor.matmul_mx(
                        out=mm[:, P * t : P * t + P],
                        lhsT=zrq[g][:, ch].bitcast(FP8X4),
                        lhsT_scale=zrs[g][:, ch],
                        rhs=codes[:, dcol].bitcast(FP8X4),
                        rhs_scale=scales[:, dcol],
                        start=(g == 0),
                        stop=(g == 1),
                    )
            res = work.tile([P, 512], F32, name="res", bufs=6, align_bytes=64)
            copy(out=res[:], in_=mm[:])
            nc.sync.dma_start(
                out=out_0[512 * G : 512 * G + 512, col : col + P].rearrange("(p t) m -> p t m", t=4),
                in_=res[:].rearrange("p (t m) -> p t m", t=4),
            )
            og = work.tile([P, 512], BF16, name="og", bufs=6, align_bytes=64)
            og_v = og[:].rearrange("p (m t) -> p m t", t=4)
            if how == "A":
                nc.scalar.copy(out=og_v, in_=mm[:].rearrange("p (t m) -> p m t", t=4))
            if (hc, G) not in ow:
                ow[hc, G] = work.tile([P, 3 * P], U32, name="ow", bufs=4, align_bytes=64)
                done[hc, G] = 0
            words = ow[hc, G]

            def cast():
                res_v = res[:].rearrange("p (t m) -> p m t", t=4)
                if how == "V":
                    nc.vector.tensor_copy(out=og_v, in_=res_v)
                if how == "G":
                    nc.gpsimd.tensor_scalar(
                        out=og_v, in0=res_v, scalar1=1.0, scalar2=1.0, op0=ALU.mult, op1=ALU.mult
                    )

            def plane():
                nc.vector.quantize_mx(
                    out=words[:, gate * P : gate * P + P].bitcast(FP8X4),
                    scales=osc[:, G, col : col + P],
                    in_=og[:],
                )
                done[hc, G] += 1
                if done[hc, G] == 3:
                    store_words(hc, G)

            pending.append((how, cast, plane))

        def take_pending(n=99):
            got = list(pending[:n])
            rest = list(pending[n:])
            pending.clear()
            pending.extend(rest)
            return got

        dhq = keep.tile([P, 2, 4, HID], BF16, name="dhq", align_bytes=64)

        def quarter_dh(g):
            nc.vector.tensor_scalar_mul(out=dhq[:, g], in0=dh_sb[:, g], scalar1=0.25)

        nc.scalar.copy(out=r_f[:], in_=r_t[:].rearrange("p g t -> p (g t)"))
        U = [0, 2, 1, 3, 4, 5, 6, 7]
        first = {GG: gate_bank(), GO: gate_bank(), GF: psum.tile([P, 512], F32, name="first_f", tag="tp3", bufs=1)}
        slots = [("s2", 2), ("s2", 2), ("tp0", 1), ("tp1", 1)]
        banks = [za_turn(0, t, *slots[t]) for t in range(4)]
        for t in range(4):
            za_mul(0, t, banks[t])
            zr_scale(0, t)
            za_quant_slice(0, t)
        make_bias()
        for t in range(4):
            for gate in (GG, GO, GF):
                gate_pass(first[gate], U[0], gate, slice(P * t, P * t + P))
        for gate in (GG, GO, GF):
            gate_act(U[0], gate, first[gate])
        square_g(U[0])
        turn(U[0])
        gates(U[1])
        square_g(U[1])
        joins = [zr_join(0, 0), zr_join(0, 1)]
        quarter_dh(0)
        zr_quant(0, 0, joins[0])
        phase_a(U[0])
        zr10 = zr_new()
        zr_mul_piece(1, 0, 0, zr10)
        for t in range(4):
            za_mul(1, t, za_turn(1, t, "s2", 2))
            if t % 2:
                za_quant(1, t // 2)
        cell_tanh(U[0])
        cell_square(U[0])
        turn(U[1])
        turn_gate(U[0], GSQ)
        nc.scalar.activation(out=dhq[:, 1], in_=dh_sb[:, 1], func=ACTF.Copy, scale=0.25)
        gates(U[2])
        square_g(U[2])

        hows = "GAVAAA"
        BANKS = [(hc, G, gate) for hc in range(3) for G in range(2) for gate in (GO, GG, GF)]
        SPLIT = (0, 0, 0, 0, 2, 6, 10, 14, 18)
        for i in range(1, 8):
            banks = BANKS[SPLIT[i] : SPLIT[i + 1]]
            nxt = U[i + 2] if i + 2 < 8 else None
            phase_y_and_gp(U[i - 1])
            phase_a(U[i])
            dpg = delta_g(U[i - 1])
            if i == 1:
                zr_quant(0, 1, joins[1])
            if i < 4:
                zr_mul_piece(1, 0, i, zr10)
            if i == 3:
                zr11 = zr_join(1, 1)
            phase_b(U[i - 1], dpg, take_pending())
            if i == 3:
                zr_quant(1, 0, zr10)
                zr_quant(1, 1, zr11)
            if nxt and i > 2:
                gate_mm(nxt, GG)
            if i >= 4:
                out_bank(*banks[0], hows[0])
            cell_tanh(U[i])
            cell_square(U[i])
            if nxt and i <= 2:
                gate_mm(nxt, GG)
            if nxt:
                gate_mm(nxt, GO)
            if i >= 4:
                out_bank(*banks[1], hows[1])
            if i < 7:
                turn(U[i + 1])
            turn_gate(U[i], GSQ)
            if nxt:
                gate_mm(nxt, GF)
                square_g(nxt)
            if i in (1, 2):
                zr_scale(1, 2 * i - 2, 1)
                zr_scale(1, 2 * i - 1, 1)
            for k in range(2 if i >= 4 else 0, len(banks)):
                out_bank(*banks[k], hows[k])
        phase_b_last(7)
        fill = take_pending()
        spare = {
            (GO, 0): ("s2", 2),
            (GO, 1): ("s2", 2),
            (GG, 0): ("tp0", 1),
            (GG, 1): ("tp1", 1),
            (GF, 0): ("tp2", 1),
            (GF, 1): ("s1", 2),
        }

        def finish(batch):
            for how, cast, plane in batch:
                if how != "A":
                    cast()
            for how, cast, plane in batch:
                plane()

        for gate in (GO, GG, GF):
            out_bank(3, 0, gate, "A", *spare[gate, 0])
            out_bank(3, 1, gate, "V", *spare[gate, 1], nc.vector.tensor_copy)
            if gate == GO:
                finish(fill)
            finish(take_pending())
        for q in range(4):
            nc.sync.dma_start(
                out=out_2[:, 4 * q : 4 * q + 4, :].rearrange("g r m -> r g m").bitcast(I32),
                in_=osc[32 * q : 32 * q + 4, :, :].bitcast(I32),
            )
